import numpy as np
import ml_dtypes


def mxq(x, axis, fmt="e4m3"):
    dtype, down = {"e4m3": (ml_dtypes.float8_e4m3fn, 7), "e5m2": (ml_dtypes.float8_e5m2, 14)}[fmt]
    v = np.moveaxis(np.asarray(x, np.float32).astype(ml_dtypes.bfloat16).astype(np.float64), axis, -1)
    blocks = v.reshape(v.shape[:-1] + (-1, 32))
    amax = np.abs(blocks).max(-1, keepdims=True)
    byte = np.maximum(np.where(amax > 0, np.frexp(amax)[1] - 1 + 127, 0) - down, 1)
    scale = np.exp2(byte - 127.0)
    codes = (blocks / scale).astype(np.float32).astype(dtype).astype(np.float64)
    return np.moveaxis((codes * scale).reshape(v.shape), -1, axis)


WIDE = False


def mx_kscale(k):
    if not WIDE:
        return np.ones(k)
    levels = np.array([10, -10, 5, -5, 0])
    if k % 512:
        return np.exp2(np.random.permutation(np.resize(levels, k // 32))).repeat(32)
    a = np.empty((k // 512, 16))
    for p in range(k // 512):
        a[p, :8] = np.random.permutation(np.resize(levels, 8))
        for g in range(8):
            far = levels[np.abs(levels - a[p, g]) >= 10]
            a[p, g + 8] = far[np.random.randint(len(far))]
    return np.exp2(a.ravel()).repeat(32)


def f64(x):
    return np.asarray(x).astype(np.float64)


def striped(idx):
    return np.tile(idx.reshape(-1, 16).T, (8, 1)).astype(np.uint16)


def unstriped(offs):
    return offs[:16].T.reshape(-1).astype(np.int64)


def silu(v):
    return v / (1.0 + np.exp(-np.maximum(v, -700.0)))


K, T, E, C, H, N = 1024, 768, 6, 128, 1024, 256


def by_expert(wq, xq):
    return np.concatenate([wq[e].T @ xq[:, e * C:(e + 1) * C] for e in range(E)], axis=1)


def setup_inputs():
    n = np.random.standard_normal
    s = mx_kscale(K)[:, None]
    u = mx_kscale(H)
    return {
        "xT": (n((K, T)) * s).astype(np.float32),
        "w1": (n((E, K, H)) / np.sqrt(K) / s[None] * u[None, None, :]).astype(np.float32),
        "w2": (n((E, H, N)) / np.sqrt(H) / u[None, :, None]).astype(np.float32),
        "gate": np.tile(np.random.uniform(0.2, 1.0, E * C), (N, 1)).astype(np.float32),
        "offs": striped(np.random.permutation(T)[:E * C]),
    }


def reference(xT, w1, w2, gate, offs):
    idx = unstriped(offs)
    xq = mxq(f64(xT)[:, idx], 0, "e4m3")
    h = silu(by_expert(mxq(f64(w1), 1, "e4m3"), xq))
    y = by_expert(mxq(f64(w2), 1, "e4m3"), mxq(h, 0, "e4m3"))
    out = np.zeros((N, T))
    out[:, idx] = f64(gate) * y
    return out

from contextlib import ExitStack

import concourse.mybir as mybir

K, T, E, C, H, N = 1024, 768, 6, 128, 1024, 256
FLOPS = 2 * K * H * E * C + 2 * H * N * E * C

F32 = mybir.dt.float32
BF16 = mybir.dt.bfloat16
U32 = mybir.dt.uint32
U16 = mybir.dt.uint16
U8 = mybir.dt.uint8
FP8X4 = mybir.dt.float8_e4m3fn_x4
MULT = mybir.AluOpType.mult
SILU = mybir.ActivationFunctionType.Silu

P = 128
PACK = 4
PASS = P * PACK
G = K // PASS
HB = H // PASS
NB = N // P


def tile_routed_moe_kernel(tc, xT, w1, w2, gate, offs, out):
    nc = tc.nc
    xT_v = xT.rearrange("(g p j) t -> g p j t", p=P, j=PACK)
    w1_v = w1.rearrange("e (g p j) c -> e g p j c", p=P, j=PACK)
    w2_v = w2.rearrange("e (g p j) c -> e g p j c", p=P, j=PACK)
    out_v = out.rearrange("(b p) t -> b p t", p=P)

    with ExitStack() as ctx:
        keep = ctx.enter_context(tc.tile_pool(name="keep", bufs=1))
        raws = ctx.enter_context(tc.tile_pool(name="raws", bufs=6))
        raws2 = ctx.enter_context(tc.tile_pool(name="raws2", bufs=4))
        grp = ctx.enter_context(tc.tile_pool(name="grp", bufs=3))
        cod = ctx.enter_context(tc.tile_pool(name="cod", bufs=8))
        hid = ctx.enter_context(tc.tile_pool(name="hid", bufs=3))
        psum_a = ctx.enter_context(tc.psum_pool(name="psum_a", bufs=4))
        psum_y = ctx.enter_context(tc.psum_pool(name="psum_y", bufs=2))

        warm_in = keep.tile([P, 1], F32, name="warm_in")
        warm_out = keep.tile([P, 1], F32, name="warm_out")
        nc.vector.memset(warm_in[:], 0.0)
        nc.scalar.activation(warm_out[:], warm_in[:], SILU)

        offsets = keep.tile([P, E * C // 16], U16, name="offsets")
        gate_sb = keep.tile([P, NB, E * C], F32, name="gate_sb")
        xw = [keep.tile([P, T], U32, name=f"xw{g}", align_bytes=64) for g in range(G)]
        xs = [keep.tile([P, T], U8, name=f"xs{g}", align_bytes=64) for g in range(G)]
        gw = keep.tile([P, G, E * C], U32, name="gw", align_bytes=64)
        gs = keep.tile([P, G, E * C], U8, name="gs", align_bytes=64)
        window = [keep.tile([P, T], F32, name=f"window{b}") for b in range(NB)]

        for g in range(G):
            nc.gpsimd.memset(xs[g][:], 0)

        for g in range(G):
            raw = raws.tile([P, PACK, T], F32, name="raw_x", tag="raw")
            nc.sync.dma_start(out=raw[:], in_=xT_v[g])
            if g == G - 1:
                nc.sync.dma_start(offsets[:], offs)
            for t0, t1, copy in ((0, 512, nc.vector.tensor_copy), (512, 768, nc.scalar.copy)):
                grouped = grp.tile([P, (t1 - t0) * PACK], BF16, name=f"grp_x{t0}", align_bytes=64)
                copy(
                    out=grouped[:].rearrange("p (c i j) -> p c j i", i=4, j=PACK),
                    in_=raw[:, :, t0:t1].rearrange("p j (c i) -> p c j i", i=4),
                )
                nc.vector.quantize_mx(
                    out=xw[g][:, t0:t1].bitcast(FP8X4), scales=xs[g][:, t0:t1], in_=grouped[:]
                )
        half = E * C // 2
        for s in range(2):
            for g in range(G):
                sl = offsets[:, s * half // 16 : (s + 1) * half // 16]
                nc.vector.tensor_copy(out=gw[:, g, s * half : (s + 1) * half], in_=xw[g][:].indirect(sl))
                nc.vector.tensor_copy(out=gs[:, g, s * half : (s + 1) * half], in_=xs[g][:].indirect(sl))

        w1q = {}
        w2q = {}

        def load_w1(e):
            for g in range(G):
                raw = raws.tile([P, PACK, H], F32, name="raw_w1", tag="raw")
                last = e == E - 1 and g == G - 1
                for c0 in range(0, H, PASS if last else H):
                    c1 = c0 + (PASS if last else H)
                    nc.sync.dma_start(out=raw[:, :, c0:c1], in_=w1_v[e, g][:, :, c0:c1])
                for h in range(HB):
                    grouped = grp.tile([P, PASS * PACK], BF16, name=f"grp_w1_{h}", align_bytes=64)
                    dst = grouped[:].rearrange("p (t m j) -> p m j t", t=PACK, j=PACK)
                    src = raw[:, :, h * PASS : (h + 1) * PASS].rearrange("p j (m t) -> p m j t", t=PACK)
                    cut = 48 if last else (P if h == 0 else 0)
                    if cut > 0:
                        nc.scalar.copy(out=dst[:, :cut], in_=src[:, :cut])
                    if cut < P:
                        nc.vector.tensor_copy(out=dst[:, cut:], in_=src[:, cut:])
                    codes = cod.tile([P, PASS], U32, name="w1_codes", align_bytes=64)
                    scales = cod.tile([P, PASS], U8, name="w1_scales", align_bytes=64)
                    nc.vector.quantize_mx(out=codes[:].bitcast(FP8X4), scales=scales[:], in_=grouped[:])
                    w1q[e, g, h] = (codes, scales)

        def load_w2(e):
            codes = hid.tile([P, HB, N], U32, name="w2_codes", align_bytes=64)
            scales = hid.tile([P, HB, N], U8, name="w2_scales", align_bytes=64)
            for h in range(HB):
                raw = raws2.tile([P, PACK, N], F32, name="raw_w2")
                nc.sync.dma_start(out=raw[:], in_=w2_v[e, h])
                grouped = grp.tile([P, N * PACK], BF16, name="grp_w2", align_bytes=64)
                dst = grouped[:].rearrange("p (c i j) -> p c j i", i=4, j=PACK)
                src = raw[:].rearrange("p j (c i) -> p c j i", i=4)
                cut = 24 if e == E - 1 and h == HB - 1 else N // 4
                if cut > 0:
                    nc.scalar.copy(out=dst[:, :cut], in_=src[:, :cut])
                if cut < N // 4:
                    nc.vector.tensor_copy(out=dst[:, cut:], in_=src[:, cut:])
                nc.vector.quantize_mx(out=codes[:, h, :].bitcast(FP8X4), scales=scales[:, h, :], in_=grouped[:])
            w2q[e] = (codes, scales)

        hq = {}

        def layer1(e):
            slots = slice(e * C, (e + 1) * C)
            grouped = hid.tile([P, HB, C * PACK], BF16, name="grp_h", align_bytes=64)
            for h in range(HB):
                acc = psum_a.tile([P, PACK, C], F32, name="acc_a")
                for t in range(PACK):
                    for g in range(G):
                        codes, scales = w1q[e, g, h]
                        nc.tensor.matmul_mx(
                            out=acc[:, t, :],
                            lhsT=codes[:, t * P : (t + 1) * P].bitcast(FP8X4),
                            lhsT_scale=scales[:, t * P : (t + 1) * P],
                            rhs=gw[:, g, slots].bitcast(FP8X4),
                            rhs_scale=gs[:, g, slots],
                            start=(g == 0),
                            stop=(g == G - 1),
                        )
                nc.scalar.activation(
                    grouped[:, h, :].rearrange("p (n t) -> p n t", t=PACK),
                    acc[:].rearrange("p t n -> p n t"),
                    SILU,
                )
            codes = hid.tile([P, HB, C], U32, name="h_codes", align_bytes=64)
            scales = hid.tile([P, HB, C], U8, name="h_scales", align_bytes=64)
            nc.vector.quantize_mx(
                out=codes[:].rearrange("p g n -> p (g n)").bitcast(FP8X4),
                scales=scales[:].rearrange("p g n -> p (g n)"),
                in_=grouped[:].rearrange("p g n -> p (g n)"),
            )
            hq[e] = (codes, scales)

        def layer2(e):
            codes, scales = w2q[e]
            hcodes, hscales = hq[e]
            accs = [psum_y.tile([P, C], F32, name=f"acc_y{b}") for b in range(NB)]
            for h in range(HB):
                for b in range(NB):
                    cols = slice(b * P, (b + 1) * P)
                    nc.tensor.matmul_mx(
                        out=accs[b][:],
                        lhsT=codes[:, h, cols].bitcast(FP8X4),
                        lhsT_scale=scales[:, h, cols],
                        rhs=hcodes[:, h, :].bitcast(FP8X4),
                        rhs_scale=hscales[:, h, :],
                        start=(h == 0),
                        stop=(h == HB - 1),
                    )
            y = hid.tile([P, NB, C], F32, name="y")
            for b in range(NB):
                nc.scalar.copy(out=y[:, b, :], in_=accs[b][:])
                nc.vector.tensor_tensor(
                    window[b][:].indirect(offsets[:, e * C // 16 : (e + 1) * C // 16]),
                    y[:, b, :],
                    gate_sb[:, b, e * C : (e + 1) * C],
                    MULT,
                )

        load_w1(0)
        load_w2(0)
        nc.sync.dma_start(out=gate_sb[:], in_=gate.rearrange("(b p) s -> p b s", p=P))
        for e in range(1, E):
            load_w1(e)
            layer1(e - 1)
            layer2(e - 1)
            load_w2(e)
        layer1(E - 1)
        layer2(E - 1)
        for b in range(NB):
            nc.sync.dma_start(out=out_v[b], in_=window[b][:])
